import numpy as np, ml_dtypes
CORES = [211,219,227,235,243,251,83,91,99,107,115,123]
N = 12
KT, FB, TK = 1, 128, 128
def setup_inputs(rng):
    return {"x": rng.standard_normal((N, 128, KT * TK), dtype=np.float32).astype(ml_dtypes.bfloat16), "w": rng.standard_normal((N, 128, KT * N * FB), dtype=np.float32).astype(ml_dtypes.bfloat16)}
def setup_inputs_big(rng):
    d = setup_inputs(rng)
    for k in ("x", "w"): d[k] = (d[k].astype(np.float32) * 1024.0).astype(d[k].dtype)
    return d
def setup_inputs_small(rng):
    d = setup_inputs(rng)
    for k in ("x", "w"): d[k] = (d[k].astype(np.float32) * (1 / 1024.0)).astype(d[k].dtype)
    return d
def setup_inputs_apart(rng):
    d = setup_inputs(rng)
    f = (10.0 ** rng.permutation(np.linspace(-1.5, 1.5, N))).astype(np.float32).reshape(N, 1, 1)
    for k in ("x", "w"): d[k] = (d[k].astype(np.float32) * f).astype(d[k].dtype)
    return d
def reference(x, w):
    X, W = x.astype(np.float64), w.astype(np.float64)
    y = np.zeros((N, FB, N * TK))
    for j in range(N):
        for r in range(N):
            for t in range(KT):
                y[r][:, TK * j:TK * j + TK] += W[j][:, FB * (N * t + r):FB * (N * t + r) + FB].T @ X[j][:, TK * t:TK * t + TK]
    return {"y": y.astype(ml_dtypes.bfloat16 if x.dtype != np.float64 else np.float64)}

@@ -1,0 +1,189 @@
+B = 128
+
+SENDS = [
+    ("direct", [3, 4]),
+    ("far", [1, 11, 9]),
+    ("far", [2, 10]),
+    ("far", [8]),
+    ("direct", [5, 6, 7]),
+]
+CHUNKS = [[3, 4], [1, 11, 9], [2, 10, 8], [5, 6, 7], [0]]
+LOADS = [("scalar", [3, 4]), ("sync", [8, 9, 10, 11]), ("scalar", [0, 1, 2]), ("sync", [5, 6, 7])]
+STORES = [("sync", [3, 4, 5]), ("scalar", [10, 11, 0, 1, 2]), ("sync", [6, 7, 8, 9])]
+FEED_ALL_ENGINES = False
+
+_N = 12
+SCRATCH = {
+    "xs": ("sbuf", [128, B], "bfloat16"),
+    "ws": ("sbuf", [128, _N * B], "bfloat16"),
+    "out": ("sbuf", [128, (_N - 1) * B], "bfloat16"),
+    "land": ("sbuf", [128, _N * B], "bfloat16"),
+}
+for _c in range(len(CHUNKS)):
+    SCRATCH["ps%d" % _c] = ("psum", [128, 512], "float32")
+SEMAPHORES = (["ldx", "own", "fed", "sent", "st_sync", "st_scalar"]
+              + ["ld%d" % i for i in range(len(LOADS))]
+              + ["mm%d" % c for c in range(len(CHUNKS))]
+              + ["cp%d" % c for c in range(len(CHUNKS))]
+              + ["arr%d" % s for s in range(len(STORES))])
+
+_POS = {}
+for _ks in CHUNKS:
+    for _k in _ks:
+        if _k != 0:
+            _POS[_k] = len(_POS)
+_CHUNK_OF = {k: c for c, ks in enumerate(CHUNKS) for k in ks}
+_STORE_OF = {k: s for s, (_q, ks) in enumerate(STORES) for k in ks}
+
+
+def _count(mask):
+    return bin(mask).count("1")
+
+
+def _runs(blocks):
+    runs = []
+    for b in sorted(blocks):
+        if runs and runs[-1][1] == b:
+            runs[-1][1] = b + 1
+        else:
+            runs.append([b, b + 1])
+    return runs
+
+
+def _cols(first, past):
+    return slice(first * B, past * B)
+
+
+def _lanes(T, topo, rc):
+    cores = list(T.cores)
+    n = len(cores)
+    j = cores.index(rc)
+    span = topo.CORES_PER_CHIP
+    idle = [c for c in range(max(0, rc - span), rc + span)
+            if topo.host(c) == topo.host(rc) and topo.chip(c) == topo.chip(rc) and c not in cores]
+    idle.sort(key=lambda c: sum(1 for d in cores if topo.may_write(c, d)))
+    lanes = []
+    for where, ks in SENDS:
+        if where == "direct":
+            lanes.append(rc)
+            continue
+        fit = [c for c in idle if c not in lanes
+               and (topo.die(c) != topo.die(rc)) == (where == "far")
+               and all(topo.may_write(c, cores[(j + k) % n]) for k in ks)]
+        lanes.append(fit[0])
+    return lanes
+
+
+def _feed_mask(T, topo, rc, helper):
+    on_chip = topo.mask(rc, helper)
+    if FEED_ALL_ENGINES:
+        return on_chip
+    leaving = 0
+    for d in T.cores:
+        if d != rc:
+            leaving |= topo.mask(rc, d)
+    return (on_chip & ~leaving) or on_chip
+
+
+def _send(g, T, topo, core, j, k):
+    cores = list(T.cores)
+    d = cores[(j + k) % len(cores)]
+    rid, pid = topo.addr(d, core)
+    mask = topo.mask(core, d)
+    g.remote_dma(out_ap=T.land[:, _cols(j, j + 1)], in_ap=T.out[:, _cols(_POS[k], _POS[k] + 1)],
+                 remote_sem=T.sem["arr%d" % _STORE_OF[k]], local_sem=T.sem.sent,
+                 pid=pid, routing_id=rid, dma_engine_mask=mask)
+    return _count(mask)
+
+
+def _helper_program(g, core, T, topo):
+    for rc in T.cores:
+        if topo.host(rc) != topo.host(core) or topo.chip(rc) != topo.chip(core):
+            continue
+        lanes = _lanes(T, topo, rc)
+        if core not in lanes:
+            continue
+        ks = SENDS[lanes.index(core)][1]
+        g.wait_ge(T.sem.fed, _count(_feed_mask(T, topo, rc, core)))
+        sent = 0
+        for k in ks:
+            sent += _send(g, T, topo, core, T.rank_of(rc), k)
+        g.wait_ge(T.sem.sent, sent)
+
+
+def rank_program(g, core, T, topo):
+    rank = T.rank_of(core)
+    if rank is None:
+        _helper_program(g, core, T, topo)
+        return
+    cores = list(T.cores)
+    n = len(cores)
+    queue = {"sync": g.sync, "scalar": g.scalar}
+
+    g.sync.dma_start(out=T.xs[:], in_=T.x[:]).then_inc(T.sem.ldx, 16)
+    loaded = []
+    for i, (q, ks) in enumerate(LOADS):
+        runs = _runs((rank + k) % n for k in ks)
+        for a, b in runs:
+            queue[q].dma_start(out=T.ws[:, _cols(a, b)], in_=T.w[:, _cols(a, b)]).then_inc(T.sem["ld%d" % i], 16)
+        loaded.append(16 * len(runs))
+
+    g.tensor.wait_ge(T.sem.ldx, 16)
+    have = []
+    for c, ks in enumerate(CHUNKS):
+        for i, (_q, lks) in enumerate(LOADS):
+            if i not in have and any(k in lks for k in ks):
+                g.tensor.wait_ge(T.sem["ld%d" % i], loaded[i])
+                have.append(i)
+        for p, k in enumerate(ks):
+            r = (rank + k) % n
+            g.tensor.matmul(out=T["ps%d" % c][:, _cols(p, p + 1)], lhsT=T.ws[:, _cols(r, r + 1)], rhs=T.xs[:],
+                            start=True, stop=True).then_inc(T.sem["mm%d" % c], 1)
+
+    for c, ks in enumerate(CHUNKS):
+        g.vector.wait_ge(T.sem["mm%d" % c], len(ks))
+        if ks == [0]:
+            g.vector.tensor_copy(out=T.land[:, _cols(rank, rank + 1)], in_=T["ps%d" % c][:, _cols(0, 1)]).then_inc(T.sem.own, 1)
+        else:
+            p = _POS[ks[0]]
+            g.vector.tensor_copy(out=T.out[:, _cols(p, p + len(ks))],
+                                 in_=T["ps%d" % c][:, _cols(0, len(ks))]).then_inc(T.sem["cp%d" % c], 1)
+
+    lanes = _lanes(T, topo, core)
+    ready = []
+    sent = 0
+    for (where, ks), lane in zip(SENDS, lanes):
+        for k in ks:
+            c = _CHUNK_OF[k]
+            if c not in ready:
+                g.wait_ge(T.sem["cp%d" % c], 1)
+                ready.append(c)
+        if lane == core:
+            for k in ks:
+                sent += _send(g, T, topo, core, rank, k)
+        else:
+            piece = _cols(_POS[ks[0]], _POS[ks[0]] + len(ks))
+            rid, pid = topo.addr(lane, core)
+            mask = _feed_mask(T, topo, core, lane)
+            g.remote_dma(out_ap=T.out[:, piece], in_ap=T.out[:, piece], remote_sem=T.sem.fed, local_sem=T.sem.sent,
+                         pid=pid, routing_id=rid, dma_engine_mask=mask)
+            sent += _count(mask)
+    g.wait_ge(T.sem.sent, sent)
+
+    stored = {"sync": 0, "scalar": 0}
+    for s, (q, ks) in enumerate(STORES):
+        due = 0
+        for k in ks:
+            if k == 0:
+                queue[q].wait_ge(T.sem.own, 1)
+                continue
+            src = cores[(rank - k) % n]
+            sender = [lane for (_w, lks), lane in zip(SENDS, _lanes(T, topo, src)) if k in lks][0]
+            due += _count(topo.mask(sender, core))
+        queue[q].wait_ge(T.sem["arr%d" % s], due)
+        for a, b in _runs((rank - k) % n for k in ks):
+            queue[q].dma_start(out=T.y[:, _cols(a, b)], in_=T.land[:, _cols(a, b)]).then_inc(T.sem["st_" + q], 16)
+            stored[q] += 16
+    for q in stored:
+        if stored[q]:
+            queue[q].wait_ge(T.sem["st_" + q], stored[q])

@@ -1,15 +1,17 @@
+from concourse.bass import DstId, RemoteDMATransfer
+
 B = 128
 
 SENDS = [
-    ("direct", [3, 4]),
-    ("far", [1, 11, 9]),
-    ("far", [2, 10]),
-    ("far", [8]),
-    ("direct", [5, 6, 7]),
+    ("direct", [1], "seq"),
+    ("far", [2, 3], "fused"),
+    ("far+", [4, 5], "fused"),
+    ("direct", [6, 7, 8, 9], "fused"),
+    ("direct", [10, 11], "fused"),
 ]
-CHUNKS = [[3, 4], [1, 11, 9], [2, 10, 8], [5, 6, 7], [0]]
-LOADS = [("scalar", [3, 4]), ("sync", [8, 9, 10, 11]), ("scalar", [0, 1, 2]), ("sync", [5, 6, 7])]
-STORES = [("sync", [3, 4, 5]), ("scalar", [10, 11, 0, 1, 2]), ("sync", [6, 7, 8, 9])]
+CHUNKS = [[1], [2, 3, 4, 5], [6, 7, 8, 9], [10, 11], [0]]
+LOADS = [("scalar", [1]), ("sync", [2, 3, 4, 5]), ("scalar", [6, 7, 8, 9]), ("sync", [10, 11, 0])]
+STORES = [("sync", [6, 7, 8, 9]), ("scalar", [0, 1]), ("scalar", [2, 3, 4, 5]), ("sync", [10, 11])]
 FEED_ALL_ENGINES = False
 
 _N = 12
@@ -40,6 +42,14 @@ def _count(mask):
     return bin(mask).count("1")
 
 
+def _share(mask, parts):
+    bits = [1 << i for i in range(mask.bit_length()) if (mask >> i) & 1]
+    each = 1
+    while each * 2 * parts <= len(bits):
+        each *= 2
+    return [sum(bits[p * each:(p + 1) * each]) for p in range(parts)]
+
+
 def _runs(blocks):
     runs = []
     for b in sorted(blocks):
@@ -63,37 +73,70 @@ def _lanes(T, topo, rc):
             if topo.host(c) == topo.host(rc) and topo.chip(c) == topo.chip(rc) and c not in cores]
     idle.sort(key=lambda c: sum(1 for d in cores if topo.may_write(c, d)))
     lanes = []
-    for where, ks in SENDS:
+    for where, ks, _how in SENDS:
         if where == "direct":
             lanes.append(rc)
             continue
         fit = [c for c in idle if c not in lanes
-               and (topo.die(c) != topo.die(rc)) == (where == "far")
+               and (topo.die(c) != topo.die(rc)) == where.startswith("far")
                and all(topo.may_write(c, cores[(j + k) % n]) for k in ks)]
         lanes.append(fit[0])
     return lanes
 
 
-def _feed_mask(T, topo, rc, helper):
-    on_chip = topo.mask(rc, helper)
-    if FEED_ALL_ENGINES:
-        return on_chip
+def _feeds(T, topo, rc, lanes):
     leaving = 0
     for d in T.cores:
         if d != rc:
             leaving |= topo.mask(rc, d)
-    return (on_chip & ~leaving) or on_chip
+    calls = []
+    for i, (where, _ks, _how) in enumerate(SENDS):
+        if where == "direct":
+            continue
+        if where.endswith("+"):
+            calls[-1].append(i)
+        else:
+            calls.append([i])
+    out = []
+    for call in calls:
+        mask = topo.mask(rc, lanes[call[0]])
+        for i in call:
+            mask &= topo.mask(rc, lanes[i])
+        if not FEED_ALL_ENGINES and mask & ~leaving:
+            mask &= ~leaving
+        out.append(list(zip(call, _share(mask, len(call)))))
+    return out
 
 
-def _send(g, T, topo, core, j, k):
+def _send_masks(T, topo, sender, j, i):
     cores = list(T.cores)
-    d = cores[(j + k) % len(cores)]
-    rid, pid = topo.addr(d, core)
-    mask = topo.mask(core, d)
-    g.remote_dma(out_ap=T.land[:, _cols(j, j + 1)], in_ap=T.out[:, _cols(_POS[k], _POS[k] + 1)],
-                 remote_sem=T.sem["arr%d" % _STORE_OF[k]], local_sem=T.sem.sent,
-                 pid=pid, routing_id=rid, dma_engine_mask=mask)
-    return _count(mask)
+    _where, ks, how = SENDS[i]
+    mask = topo.mask(sender, cores[(j + ks[0]) % len(cores)])
+    for k in ks:
+        mask &= topo.mask(sender, cores[(j + k) % len(cores)])
+    if how == "fused":
+        return dict(zip(ks, _share(mask, len(ks))))
+    return {k: mask for k in ks}
+
+
+def _send(g, T, topo, core, j, i):
+    cores = list(T.cores)
+    _where, ks, how = SENDS[i]
+    masks = _send_masks(T, topo, core, j, i)
+    transfers = []
+    for k in ks:
+        rid, pid = topo.addr(cores[(j + k) % len(cores)], core)
+        src, dst = T.out[:, _cols(_POS[k], _POS[k] + 1)], T.land[:, _cols(j, j + 1)]
+        sem = T.sem["arr%d" % _STORE_OF[k]]
+        if how == "fused":
+            transfers.append(RemoteDMATransfer(dst_ids=[DstId(rid=rid, pnc=pid)], dma_engine_mask=masks[k], remote_sem=sem,
+                                               src=src, dst=dst))
+        else:
+            g.remote_dma(out_ap=dst, in_ap=src, remote_sem=sem, local_sem=T.sem.sent,
+                         pid=pid, routing_id=rid, dma_engine_mask=masks[k])
+    if transfers:
+        g.remote_dma_fused(transfers, local_sem=T.sem.sent)
+    return sum(_count(m) for m in masks.values())
 
 
 def _helper_program(g, core, T, topo):
@@ -103,12 +146,12 @@ def _helper_program(g, core, T, topo):
         lanes = _lanes(T, topo, rc)
         if core not in lanes:
             continue
-        ks = SENDS[lanes.index(core)][1]
-        g.wait_ge(T.sem.fed, _count(_feed_mask(T, topo, rc, core)))
-        sent = 0
-        for k in ks:
-            sent += _send(g, T, topo, core, T.rank_of(rc), k)
-        g.wait_ge(T.sem.sent, sent)
+        mine = lanes.index(core)
+        for call in _feeds(T, topo, rc, lanes):
+            for i, mask in call:
+                if i == mine:
+                    g.wait_ge(T.sem.fed, _count(mask))
+        g.wait_ge(T.sem.sent, _send(g, T, topo, core, T.rank_of(rc), mine))
 
 
 def rank_program(g, core, T, topo):
@@ -150,24 +193,31 @@ def rank_program(g, core, T, topo):
                                  in_=T["ps%d" % c][:, _cols(0, len(ks))]).then_inc(T.sem["cp%d" % c], 1)
 
     lanes = _lanes(T, topo, core)
+    feeds = {call[0][0]: call for call in _feeds(T, topo, core, lanes)}
     ready = []
     sent = 0
-    for (where, ks), lane in zip(SENDS, lanes):
+
+    def need(ks):
         for k in ks:
-            c = _CHUNK_OF[k]
-            if c not in ready:
-                g.wait_ge(T.sem["cp%d" % c], 1)
-                ready.append(c)
-        if lane == core:
-            for k in ks:
-                sent += _send(g, T, topo, core, rank, k)
-        else:
-            piece = _cols(_POS[ks[0]], _POS[ks[0]] + len(ks))
-            rid, pid = topo.addr(lane, core)
-            mask = _feed_mask(T, topo, core, lane)
-            g.remote_dma(out_ap=T.out[:, piece], in_ap=T.out[:, piece], remote_sem=T.sem.fed, local_sem=T.sem.sent,
-                         pid=pid, routing_id=rid, dma_engine_mask=mask)
-            sent += _count(mask)
+            if _CHUNK_OF[k] not in ready:
+                g.wait_ge(T.sem["cp%d" % _CHUNK_OF[k]], 1)
+                ready.append(_CHUNK_OF[k])
+
+    for i, (where, ks, _how) in enumerate(SENDS):
+        if where == "direct":
+            need(ks)
+            sent += _send(g, T, topo, core, rank, i)
+        elif i in feeds:
+            transfers = []
+            for f, mask in feeds[i]:
+                fks = SENDS[f][1]
+                need(fks)
+                piece = _cols(_POS[fks[0]], _POS[fks[0]] + len(fks))
+                rid, pid = topo.addr(lanes[f], core)
+                transfers.append(RemoteDMATransfer(dst_ids=[DstId(rid=rid, pnc=pid)], dma_engine_mask=mask,
+                                                   remote_sem=T.sem.fed, src=T.out[:, piece], dst=T.out[:, piece]))
+                sent += _count(mask)
+            g.remote_dma_fused(transfers, local_sem=T.sem.sent)
     g.wait_ge(T.sem.sent, sent)
 
     stored = {"sync": 0, "scalar": 0}
@@ -178,8 +228,9 @@ def rank_program(g, core, T, topo):
                 queue[q].wait_ge(T.sem.own, 1)
                 continue
             src = cores[(rank - k) % n]
-            sender = [lane for (_w, lks), lane in zip(SENDS, _lanes(T, topo, src)) if k in lks][0]
-            due += _count(topo.mask(sender, core))
+            for i, lane in enumerate(_lanes(T, topo, src)):
+                if k in SENDS[i][1]:
+                    due += _count(_send_masks(T, topo, lane, (rank - k) % n, i)[k])
         queue[q].wait_ge(T.sem["arr%d" % s], due)
         for a, b in _runs((rank - k) % n for k in ks):
             queue[q].dma_start(out=T.y[:, _cols(a, b)], in_=T.land[:, _cols(a, b)]).then_inc(T.sem["st_" + q], 16)

@@ -4,15 +4,15 @@ B = 128
 
 SENDS = [
     ("direct", [1], "seq"),
-    ("far", [2, 3], "fused"),
-    ("far+", [4, 5], "fused"),
+    ("near", [2, 4], "fused"),
+    ("far+", [3, 5], "fused"),
     ("direct", [6, 7, 8, 9], "fused"),
     ("direct", [10, 11], "fused"),
 ]
-CHUNKS = [[1], [2, 3, 4, 5], [6, 7, 8, 9], [10, 11], [0]]
+CHUNKS = [[1], [2, 4], [3, 5], [6, 7], [8, 9], [10, 11], [0]]
 LOADS = [("scalar", [1]), ("sync", [2, 3, 4, 5]), ("scalar", [6, 7, 8, 9]), ("sync", [10, 11, 0])]
 STORES = [("sync", [6, 7, 8, 9]), ("scalar", [0, 1]), ("scalar", [2, 3, 4, 5]), ("sync", [10, 11])]
-FEED_ALL_ENGINES = False
+FEED_ALL_ENGINES = True
 
 _N = 12
 SCRATCH = {

from concourse.bass import DstId, RemoteDMATransfer

B = 128

SENDS = [
    ("direct", [1], "seq"),
    ("near", [2, 4], "fused"),
    ("far+", [3, 5], "fused"),
    ("direct", [6, 7, 8, 9], "fused"),
    ("direct", [10, 11], "fused"),
]
CHUNKS = [[1], [2, 4], [3, 5], [6, 7], [8, 9], [10, 11], [0]]
LOADS = [("scalar", [1]), ("sync", [2, 3, 4, 5]), ("scalar", [6, 7, 8, 9]), ("sync", [10, 11, 0])]
STORES = [("sync", [6, 7, 8, 9]), ("scalar", [0, 1]), ("scalar", [2, 3, 4, 5]), ("sync", [10, 11])]
FEED_ALL_ENGINES = True

_N = 12
SCRATCH = {
    "xs": ("sbuf", [128, B], "bfloat16"),
    "ws": ("sbuf", [128, _N * B], "bfloat16"),
    "out": ("sbuf", [128, (_N - 1) * B], "bfloat16"),
    "land": ("sbuf", [128, _N * B], "bfloat16"),
}
for _c in range(len(CHUNKS)):
    SCRATCH["ps%d" % _c] = ("psum", [128, 512], "float32")
SEMAPHORES = (["ldx", "own", "fed", "sent", "st_sync", "st_scalar"]
              + ["ld%d" % i for i in range(len(LOADS))]
              + ["mm%d" % c for c in range(len(CHUNKS))]
              + ["cp%d" % c for c in range(len(CHUNKS))]
              + ["arr%d" % s for s in range(len(STORES))])

_POS = {}
for _ks in CHUNKS:
    for _k in _ks:
        if _k != 0:
            _POS[_k] = len(_POS)
_CHUNK_OF = {k: c for c, ks in enumerate(CHUNKS) for k in ks}
_STORE_OF = {k: s for s, (_q, ks) in enumerate(STORES) for k in ks}


def _count(mask):
    return bin(mask).count("1")


def _share(mask, parts):
    bits = [1 << i for i in range(mask.bit_length()) if (mask >> i) & 1]
    each = 1
    while each * 2 * parts <= len(bits):
        each *= 2
    return [sum(bits[p * each:(p + 1) * each]) for p in range(parts)]


def _runs(blocks):
    runs = []
    for b in sorted(blocks):
        if runs and runs[-1][1] == b:
            runs[-1][1] = b + 1
        else:
            runs.append([b, b + 1])
    return runs


def _cols(first, past):
    return slice(first * B, past * B)


def _lanes(T, topo, rc):
    cores = list(T.cores)
    n = len(cores)
    j = cores.index(rc)
    span = topo.CORES_PER_CHIP
    idle = [c for c in range(max(0, rc - span), rc + span)
            if topo.host(c) == topo.host(rc) and topo.chip(c) == topo.chip(rc) and c not in cores]
    idle.sort(key=lambda c: sum(1 for d in cores if topo.may_write(c, d)))
    lanes = []
    for where, ks, _how in SENDS:
        if where == "direct":
            lanes.append(rc)
            continue
        fit = [c for c in idle if c not in lanes
               and (topo.die(c) != topo.die(rc)) == where.startswith("far")
               and all(topo.may_write(c, cores[(j + k) % n]) for k in ks)]
        lanes.append(fit[0])
    return lanes


def _feeds(T, topo, rc, lanes):
    leaving = 0
    for d in T.cores:
        if d != rc:
            leaving |= topo.mask(rc, d)
    calls = []
    for i, (where, _ks, _how) in enumerate(SENDS):
        if where == "direct":
            continue
        if where.endswith("+"):
            calls[-1].append(i)
        else:
            calls.append([i])
    out = []
    for call in calls:
        mask = topo.mask(rc, lanes[call[0]])
        for i in call:
            mask &= topo.mask(rc, lanes[i])
        if not FEED_ALL_ENGINES and mask & ~leaving:
            mask &= ~leaving
        out.append(list(zip(call, _share(mask, len(call)))))
    return out


def _send_masks(T, topo, sender, j, i):
    cores = list(T.cores)
    _where, ks, how = SENDS[i]
    mask = topo.mask(sender, cores[(j + ks[0]) % len(cores)])
    for k in ks:
        mask &= topo.mask(sender, cores[(j + k) % len(cores)])
    if how == "fused":
        return dict(zip(ks, _share(mask, len(ks))))
    return {k: mask for k in ks}


def _send(g, T, topo, core, j, i):
    cores = list(T.cores)
    _where, ks, how = SENDS[i]
    masks = _send_masks(T, topo, core, j, i)
    transfers = []
    for k in ks:
        rid, pid = topo.addr(cores[(j + k) % len(cores)], core)
        src, dst = T.out[:, _cols(_POS[k], _POS[k] + 1)], T.land[:, _cols(j, j + 1)]
        sem = T.sem["arr%d" % _STORE_OF[k]]
        if how == "fused":
            transfers.append(RemoteDMATransfer(dst_ids=[DstId(rid=rid, pnc=pid)], dma_engine_mask=masks[k], remote_sem=sem,
                                               src=src, dst=dst))
        else:
            g.remote_dma(out_ap=dst, in_ap=src, remote_sem=sem, local_sem=T.sem.sent,
                         pid=pid, routing_id=rid, dma_engine_mask=masks[k])
    if transfers:
        g.remote_dma_fused(transfers, local_sem=T.sem.sent)
    return sum(_count(m) for m in masks.values())


def _helper_program(g, core, T, topo):
    for rc in T.cores:
        if topo.host(rc) != topo.host(core) or topo.chip(rc) != topo.chip(core):
            continue
        lanes = _lanes(T, topo, rc)
        if core not in lanes:
            continue
        mine = lanes.index(core)
        for call in _feeds(T, topo, rc, lanes):
            for i, mask in call:
                if i == mine:
                    g.wait_ge(T.sem.fed, _count(mask))
        g.wait_ge(T.sem.sent, _send(g, T, topo, core, T.rank_of(rc), mine))


def rank_program(g, core, T, topo):
    rank = T.rank_of(core)
    if rank is None:
        _helper_program(g, core, T, topo)
        return
    cores = list(T.cores)
    n = len(cores)
    queue = {"sync": g.sync, "scalar": g.scalar}

    g.sync.dma_start(out=T.xs[:], in_=T.x[:]).then_inc(T.sem.ldx, 16)
    loaded = []
    for i, (q, ks) in enumerate(LOADS):
        runs = _runs((rank + k) % n for k in ks)
        for a, b in runs:
            queue[q].dma_start(out=T.ws[:, _cols(a, b)], in_=T.w[:, _cols(a, b)]).then_inc(T.sem["ld%d" % i], 16)
        loaded.append(16 * len(runs))

    g.tensor.wait_ge(T.sem.ldx, 16)
    have = []
    for c, ks in enumerate(CHUNKS):
        for i, (_q, lks) in enumerate(LOADS):
            if i not in have and any(k in lks for k in ks):
                g.tensor.wait_ge(T.sem["ld%d" % i], loaded[i])
                have.append(i)
        for p, k in enumerate(ks):
            r = (rank + k) % n
            g.tensor.matmul(out=T["ps%d" % c][:, _cols(p, p + 1)], lhsT=T.ws[:, _cols(r, r + 1)], rhs=T.xs[:],
                            start=True, stop=True).then_inc(T.sem["mm%d" % c], 1)

    for c, ks in enumerate(CHUNKS):
        g.vector.wait_ge(T.sem["mm%d" % c], len(ks))
        if ks == [0]:
            g.vector.tensor_copy(out=T.land[:, _cols(rank, rank + 1)], in_=T["ps%d" % c][:, _cols(0, 1)]).then_inc(T.sem.own, 1)
        else:
            p = _POS[ks[0]]
            g.vector.tensor_copy(out=T.out[:, _cols(p, p + len(ks))],
                                 in_=T["ps%d" % c][:, _cols(0, len(ks))]).then_inc(T.sem["cp%d" % c], 1)

    lanes = _lanes(T, topo, core)
    feeds = {call[0][0]: call for call in _feeds(T, topo, core, lanes)}
    ready = []
    sent = 0

    def need(ks):
        for k in ks:
            if _CHUNK_OF[k] not in ready:
                g.wait_ge(T.sem["cp%d" % _CHUNK_OF[k]], 1)
                ready.append(_CHUNK_OF[k])

    for i, (where, ks, _how) in enumerate(SENDS):
        if where == "direct":
            need(ks)
            sent += _send(g, T, topo, core, rank, i)
        elif i in feeds:
            transfers = []
            for f, mask in feeds[i]:
                fks = SENDS[f][1]
                need(fks)
                piece = _cols(_POS[fks[0]], _POS[fks[0]] + len(fks))
                rid, pid = topo.addr(lanes[f], core)
                transfers.append(RemoteDMATransfer(dst_ids=[DstId(rid=rid, pnc=pid)], dma_engine_mask=mask,
                                                   remote_sem=T.sem.fed, src=T.out[:, piece], dst=T.out[:, piece]))
                sent += _count(mask)
            g.remote_dma_fused(transfers, local_sem=T.sem.sent)
    g.wait_ge(T.sem.sent, sent)

    stored = {"sync": 0, "scalar": 0}
    for s, (q, ks) in enumerate(STORES):
        due = 0
        for k in ks:
            if k == 0:
                queue[q].wait_ge(T.sem.own, 1)
                continue
            src = cores[(rank - k) % n]
            for i, lane in enumerate(_lanes(T, topo, src)):
                if k in SENDS[i][1]:
                    due += _count(_send_masks(T, topo, lane, (rank - k) % n, i)[k])
        queue[q].wait_ge(T.sem["arr%d" % s], due)
        for a, b in _runs((rank - k) % n for k in ks):
            queue[q].dma_start(out=T.y[:, _cols(a, b)], in_=T.land[:, _cols(a, b)]).then_inc(T.sem["st_" + q], 16)
            stored[q] += 16
    for q in stored:
        if stored[q]:
            queue[q].wait_ge(T.sem["st_" + q], stored[q])
